import numpy as np
import ml_dtypes


def mxq(x, axis, fmt="e4m3"):
    dtype, down = {"e4m3": (ml_dtypes.float8_e4m3fn, 7), "e5m2": (ml_dtypes.float8_e5m2, 14)}[fmt]
    v = np.moveaxis(np.asarray(x, np.float32).astype(ml_dtypes.bfloat16).astype(np.float64), axis, -1)
    blocks = v.reshape(v.shape[:-1] + (-1, 32))
    amax = np.abs(blocks).max(-1, keepdims=True)
    byte = np.maximum(np.where(amax > 0, np.frexp(amax)[1] - 1 + 127, 0) - down, 1)
    scale = np.exp2(byte - 127.0)
    codes = (blocks / scale).astype(np.float32).astype(dtype).astype(np.float64)
    return np.moveaxis((codes * scale).reshape(v.shape), -1, axis)


WIDE = False


def mx_kscale(k):
    if not WIDE:
        return np.ones(k)
    levels = np.array([10, -10, 5, -5, 0])
    if k % 512:
        return np.exp2(np.random.permutation(np.resize(levels, k // 32))).repeat(32)
    a = np.empty((k // 512, 16))
    for p in range(k // 512):
        a[p, :8] = np.random.permutation(np.resize(levels, 8))
        for g in range(8):
            far = levels[np.abs(levels - a[p, g]) >= 10]
            a[p, g + 8] = far[np.random.randint(len(far))]
    return np.exp2(a.ravel()).repeat(32)


BF16 = ml_dtypes.bfloat16


def bf(x):
    return np.asarray(x, np.float32).astype(BF16)


def f64(x):
    return np.asarray(x).astype(np.float64)


E2M1 = np.array([0.0, 0.5, 1.0, 1.5, 2.0, 3.0, 4.0, 6.0, -0.0, -0.5, -1.0, -1.5, -2.0, -3.0, -4.0, -6.0])


def pack_weight(w, fmt):
    k, n = w.shape
    w = f64(bf(w)).reshape(k // 32, 32, n)
    amax = np.abs(w).max(1)
    if fmt == "e4m3":
        byte = np.frexp(amax)[1] - 1 + 127 - 7
    else:
        mant, ex = np.frexp(amax / 6.0)
        byte = np.where(mant > 0.5, ex, ex - 1) + 127
    byte = np.clip(np.where(amax > 0, byte, 1), 1, 254)
    scaled = (w * np.exp2(127.0 - byte)[:, None, :]).reshape(k, n).astype(np.float32)
    by_word = np.ascontiguousarray(scaled.reshape(k // 512, 128, 4, n).transpose(0, 1, 3, 2))
    if fmt == "e4m3":
        words = by_word.astype(ml_dtypes.float8_e4m3fn).view(np.uint8)
    else:
        c = by_word.astype(ml_dtypes.float4_e2m1fn).view(np.uint8) & 0xF
        words = c[..., 0::2] | (c[..., 1::2] << 4)
    return np.ascontiguousarray(words), np.ascontiguousarray(byte.astype(np.uint8).reshape(k // 512, 16, n))


def unpack_weight(words, scales, fmt):
    g, p, n, _ = words.shape
    if fmt == "e4m3":
        vals = np.ascontiguousarray(words).view(ml_dtypes.float8_e4m3fn).astype(np.float64)
    else:
        nib = np.empty((g, p, n, 4), np.uint8)
        nib[..., 0::2] = words & 0xF
        nib[..., 1::2] = words >> 4
        vals = E2M1[nib]
    vals = vals * np.repeat(np.exp2(scales.astype(np.float64) - 127.0), 8, axis=1)[..., None]
    return vals.transpose(0, 1, 3, 2).reshape(g * 512, n)
def pack4(w):
    words, scales = pack_weight(w, "e2m1")
    return words.reshape(words.shape[0], 128, -1), scales


def unpack4(words, scales):
    return unpack_weight(words.reshape(words.shape[0], 128, -1, 2), scales, "e2m1")


N, X, P, M, E, C, H = 1024, 3, 3, 512, 2, 512, 512
WIDTH2 = 0.0018


def plane_coords(pts):
    u = np.stack([pts[:, 0], pts[:, 0], pts[:, 1]], axis=0)
    v = np.stack([pts[:, 1], pts[:, 2], pts[:, 2]], axis=0)
    return u, v


def softmax_last(s):
    e = np.exp(s - np.max(s, axis=-1, keepdims=True))
    return e / np.sum(e, axis=-1, keepdims=True)


def softplus(t):
    return np.maximum(t, 0.0) + np.log(1.0 + np.exp(-np.abs(t)))


def draw0():
    sm, sc = mx_kscale(M), mx_kscale(C)
    pts = bf(np.random.uniform(0.0, 1.0, (N, X)))
    cen = bf(np.random.uniform(0.0, 1.0, (P, M, E)))
    ga = bf(np.random.standard_normal((P, M)) * sm)
    feat = bf(np.random.standard_normal((P, M, C)) * 0.106 * np.sqrt(M) / sm[None, :, None])
    gc = bf((1.0 + 0.1 * np.random.standard_normal(C)) * sc)
    w1_words, w1_scales = pack4(np.random.standard_normal((C, H)) * 2.0 / np.sqrt(C) / sc[:, None])
    b1 = bf(np.random.standard_normal(H) * 0.4)
    return {
        "pts": pts,
        "cen": cen,
        "ga": ga,
        "feat": feat,
        "gc": gc,
        "w1_words": w1_words,
        "w1_scales": w1_scales,
        "b1": b1,
    }


def core(pts, cen, ga, feat, gc, w1_words, w1_scales, b1):
    pts, cen, ga, feat, gc, b1 = f64(pts), f64(cen), f64(ga), f64(feat), f64(gc), f64(b1)
    u, v = plane_coords(pts)
    du = u[:, :, None] - cen[:, None, :, 0]
    dv = v[:, :, None] - cen[:, None, :, 1]
    d2 = du * du + dv * dv
    k = softmax_last(-d2 / WIDTH2)
    a = k * ga[:, None, :]
    f = mxq(a, 2, "e4m3") @ mxq(feat, 1, "e4m3")
    z = f[0] * f[1] * f[2] * gc[None, :]
    t = (mxq(z, 1, "e4m3") @ unpack4(w1_words, w1_scales)) + b1[None, :]
    return softplus(t)


def e4m3fn_bytes(y):
    return np.clip(np.asarray(y, np.float64), -448.0, 448.0).astype(np.float32).astype(ml_dtypes.float8_e4m3fn).view(np.uint8)


def e4m3fn_values(b):
    return np.asarray(b, np.uint8).view(ml_dtypes.float8_e4m3fn).astype(np.float64)


def setup_inputs():
    d = draw0()
    x0 = np.asarray(d['feat']).astype(np.float64)
    s = (np.max(np.abs(x0), axis=(0, 2), keepdims=True) / 448.0).astype(np.float32)
    out = {}
    for k, v in d.items():
        if k == 'feat':
            out['feat_bytes'] = e4m3fn_bytes(x0 / s.astype(np.float64))
            out['feat_scale'] = s
        else:
            out[k] = v
    return out


def reference(pts, cen, ga, feat_bytes, feat_scale, gc, w1_words, w1_scales, b1):
    return core(pts, cen, ga, e4m3fn_values(feat_bytes) * feat_scale.astype(np.float64), gc, w1_words, w1_scales, b1)

from contextlib import ExitStack

import concourse.mybir as mybir
from concourse.masks import make_identity

F32 = mybir.dt.float32
BF16 = mybir.dt.bfloat16
U32 = mybir.dt.uint32
I32 = mybir.dt.int32
U8 = mybir.dt.uint8
FP8 = mybir.dt.float8_e4m3fn
FP8X4 = mybir.dt.float8_e4m3fn_x4
FP4X4 = mybir.dt.float4_e2m1fn_x4
ACT = mybir.ActivationFunctionType
ALU = mybir.AluOpType

N, P, M, C, H = 1024, 3, 512, 512, 512
WIDTH2 = 0.0018
T_CLAMP = 40.0
FLOPS = 2 * N * M * C * P + 2 * N * C * H
COORDS = ((0, 1), (0, 2), (1, 2))
NT = N // 128
CH = 4


def tile_kplanesgaussiananchordecoder_w4_kernel(
    tc, pts, cen, ga, feat_bytes, feat_scale, gc, w1_words, w1_scales, b1, out
):
    nc = tc.nc
    with ExitStack() as ctx:
        keep = ctx.enter_context(tc.tile_pool(name="keep", bufs=1))
        work = ctx.enter_context(tc.tile_pool(name="work", bufs=2))
        ps_d2 = ctx.enter_context(tc.psum_pool(name="ps_d2", bufs=3))
        ps_xt = ctx.enter_context(tc.psum_pool(name="ps_xt", bufs=2))
        ps_f = ctx.enter_context(tc.psum_pool(name="ps_f", bufs=2))
        ps_o = ctx.enter_context(tc.psum_pool(name="ps_o", bufs=1))

        warm = keep.tile([128, 1], F32, name="warm")
        nc.vector.memset(warm[:], 0.0)
        warm2 = keep.tile([128, 1], F32, name="warm2")
        nc.scalar.activation(out=warm2[:], in_=warm[:], func=ACT.Exp)

        cenb = keep.tile([128, P, 8], BF16, name="cenb")
        nc.sync.dma_start(out=cenb[:], in_=cen.rearrange("x (p t) e -> p x (t e)", t=4))
        half = N // 2
        ptb = []
        for h in range(2):
            tile_h = keep.tile([128, half * 3], BF16, name="ptb%d" % h)
            nc.sync.dma_start(
                out=tile_h[:],
                in_=pts[h * half : (h + 1) * half, :].rearrange("n x -> (n x)").partition_broadcast(128),
            )
            ptb.append(tile_h)
        fb = keep.tile([128, P, 4, C], U8, name="fb")
        fs = keep.tile([128, 4], F32, name="fs")
        nc.sync.dma_start(out=fs[:], in_=feat_scale.rearrange("o (p t) x -> p (o t x)", t=4))
        for pl in range(P):
            nc.sync.dma_start(out=fb[:, pl, :, :], in_=feat_bytes[pl].rearrange("(p t) c -> p t c", t=4))
        ident = keep.tile([128, 128], F32, name="ident")
        make_identity(nc, ident[:])
        gab = keep.tile([128, P * M], BF16, name="gab")
        nc.gpsimd.dma_start(out=gab[:], in_=ga.rearrange("x m -> (x m)").partition_broadcast(128))
        gcb = keep.tile([128, 4], BF16, name="gcb")
        nc.gpsimd.dma_start(out=gcb[:], in_=gc.rearrange("(p t) -> p t", t=4))
        gcf = keep.tile([128, 4], F32, name="gcf")
        nc.gpsimd.tensor_copy(out=gcf[:], in_=gcb[:])
        bb = keep.tile([128, H], BF16, name="bb")
        nc.gpsimd.dma_start(out=bb[:], in_=b1.partition_broadcast(128))
        ww = keep.tile([128, 2 * H], U8, name="ww", align_bytes=64)
        ws = keep.tile([128, H], U8, name="ws", align_bytes=64)
        nc.vector.memset(ws[:].bitcast(I32), 0)
        for qd in range(4):
            nc.sync.dma_start(
                out=ws[32 * qd : 32 * qd + 4, :].bitcast(I32), in_=w1_scales[0, 4 * qd : 4 * qd + 4, :].bitcast(I32)
            )
        nc.sync.dma_start(out=ww[:], in_=w1_words[0])

        fw = [keep.tile([128, C], U32, name="fw%d" % pl, align_bytes=64) for pl in range(P)]
        fsc = [keep.tile([128, C], U8, name="fsc%d" % pl, align_bytes=64) for pl in range(P)]

        def feat_parts(pl):
            wide = work.tile([128, 4, C], BF16, name="wide", bufs=1)
            grp = work.tile([128, 4 * C], BF16, name="fgrp", bufs=1, align_bytes=64)

            def widen(t):
                nc.vector.tensor_scalar(
                    out=wide[:, t, :], in0=fb[:, pl, t, :].bitcast(FP8), scalar1=fs[:, t : t + 1], scalar2=None, op0=ALU.mult
                )

            def inter(tc2):
                nc.vector.tensor_copy(
                    out=grp[:].rearrange("p (t m j) -> p t m j", t=4, j=4)[:, 2 * tc2 : 2 * tc2 + 2],
                    in_=wide[:].rearrange("p j (m t) -> p t m j", t=4)[:, 2 * tc2 : 2 * tc2 + 2],
                )

            def quant():
                nc.vector.quantize_mx(out=fw[pl][:].bitcast(FP8X4), scales=fsc[pl][:], in_=grp[:])

            return [lambda t=t: widen(t) for t in range(4)] + [lambda: inter(0), lambda: inter(1), quant]

        steps = [(c, pl) for c in range(NT // CH) for pl in range(P)]
        jobs = [(c, pl, i) for (c, pl) in steps for i in range(CH)]
        sq = {}

        def squares(s, n0, n1, t, e):
            c, pl = steps[s]
            if s not in sq:
                sq[s] = work.tile([128, 2, 4, CH * 128], F32, name="sq")
            x = COORDS[pl][e]
            nc.scalar.activation(
                out=sq[s][:, e, t, n0:n1],
                in_=ptb[c][:].rearrange("p (n x) -> p n x", x=3)[:, n0:n1, x],
                func=ACT.Square,
                scale=-1.0,
                bias=cenb[:, pl, 2 * t + e : 2 * t + e + 1],
            )

        st = {}
        sums = {}

        def d2_min(k):
            c, pl, i = jobs[k]
            s = k // CH
            d2 = ps_d2.tile([128, 4, 128], F32, name="d2")
            for t in range(4):
                for e in range(2):
                    nc.tensor.matmul(
                        out=d2[:, t, :],
                        lhsT=sq[s][:, e, t, 128 * i : 128 * i + 128],
                        rhs=ident[:],
                        start=(e == 0),
                        stop=(e == 1),
                        is_transpose=True,
                    )
            xs = work.tile([128, M], F32, name="xs", bufs=3)
            mn = work.tile([128, 1], F32, name="mn", bufs=4)
            nc.vector.tensor_scalar(
                out=xs[:].rearrange("n (p t) -> n p t", t=4),
                in0=d2[:].rearrange("n t p -> n p t"),
                scalar1=1.0 / WIDTH2,
                scalar2=None,
                op0=ALU.mult,
                op1=ALU.min,
                accum_out=mn[:],
            )
            st[k] = [xs, mn]

        def expo(k):
            xs, mn = st[k]
            e = work.tile([128, M], F32, name="e", bufs=4)
            if k % 2 == 0:
                sums[k // 2] = work.tile([128, 2], F32, name="sm", bufs=3)
            sm = sums[k // 2]
            nc.scalar.activation(
                out=e[:], in_=xs[:], func=ACT.Exp, scale=-1.0, bias=mn[:], accum_out=sm[:, k % 2 : k % 2 + 1]
            )
            st[k] = e

        def norm(r):
            pl = jobs[2 * r][1]
            ri = work.tile([128, 2], F32, name="ri", bufs=3)
            nc.vector.reciprocal(out=ri[:], in_=sums[r][:])
            for j in range(2):
                a = work.tile([128, M], BF16, name="a", bufs=4)
                nc.vector.scalar_tensor_tensor(
                    out=a[:],
                    in0=st[2 * r + j][:],
                    scalar=ri[:, j : j + 1],
                    in1=gab[:, pl * M : (pl + 1) * M],
                    op0=ALU.mult,
                    op1=ALU.mult,
                )
                st[2 * r + j] = a

        pst = {}

        def xpose(r):
            xt = ps_xt.tile([128, 2, 2, 128], F32, name="xt")
            for j in range(2):
                words = st[2 * r + j][:].bitcast(F32)
                for u in range(2):
                    nc.tensor.transpose(xt[:, j, u, :], words[:, u : M // 2 : 2], ident[:])
            g = work.tile([128, 256 * 4], BF16, name="g", align_bytes=64)
            copy = nc.vector.tensor_copy if r % 2 == 0 else nc.scalar.copy
            copy(
                out=g[:].bitcast(F32).rearrange("p (j n u) -> p j n u", j=2, u=2),
                in_=xt[:].rearrange("p j u n -> p j n u"),
            )
            pst[r] = g

        def quant(r):
            g = pst[r]
            aw = work.tile([128, 256], U32, name="aw", align_bytes=64)
            asc = work.tile([128, 256], U8, name="asc", align_bytes=64)
            nc.vector.quantize_mx(out=aw[:].bitcast(FP8X4), scales=asc[:], in_=g[:])
            pst[r] = (aw, asc)

        fps = {}

        def mx(r, j):
            aw, asc = pst[r]
            k = 2 * r + j
            pl = jobs[k][1]
            if pl == 0:
                f = ps_f.tile([128, 2, 256], F32, name="f")
                for h in range(2):
                    t = 2 * j + h
                    nc.tensor.matmul_mx(
                        out=f[:, h, :],
                        lhsT=fw[pl][:, 128 * t : 128 * t + 128].bitcast(FP8X4),
                        lhsT_scale=fsc[pl][:, 128 * t : 128 * t + 128],
                        rhs=aw[:].bitcast(FP8X4),
                        rhs_scale=asc[:],
                        start=True,
                        stop=True,
                    )
                fps[k] = f
                return
            f = ps_f.tile([128, 4, 128], F32, name="f")
            for t in range(4):
                nc.tensor.matmul_mx(
                    out=f[:, t, :],
                    lhsT=fw[pl][:, 128 * t : 128 * t + 128].bitcast(FP8X4),
                    lhsT_scale=fsc[pl][:, 128 * t : 128 * t + 128],
                    rhs=aw[:, 128 * j : 128 * j + 128].bitcast(FP8X4),
                    rhs_scale=asc[:, 128 * j : 128 * j + 128],
                    start=True,
                    stop=True,
                )
            fps[k] = f

        zt = {}
        z1t = {}
        zg = {}

        def zmul(k):
            c, pl, i = jobs[k]
            f = fps[k]
            n = c * CH + i
            if pl == 0:
                if k % 2 == 0:
                    zt[n // 2] = work.tile([128, 4, 256], F32, name="z0", bufs=3)
                for h in range(2):
                    t = 2 * (k % 2) + h
                    nc.scalar.activation(
                        out=zt[n // 2][:, t, :], in_=f[:, h, :], func=ACT.Copy, scale=gcf[:, t : t + 1]
                    )
            elif pl == 1:
                z1 = work.tile([128, 4, 128], F32, name="z1", bufs=5)
                nc.vector.tensor_tensor(out=z1[:], in0=f[:], in1=zt[n // 2][:, :, 128 * (n % 2) : 128 * (n % 2) + 128], op=ALU.mult)
                z1t[n] = z1
            else:
                if n % 2 == 0:
                    zg[n // 2] = work.tile([128, 2, 128, 4], BF16, name="zg", align_bytes=64)
                nc.vector.tensor_tensor(
                    out=zg[n // 2][:, n % 2],
                    in0=f[:].rearrange("p t n -> p n t"),
                    in1=z1t[n][:].rearrange("p t n -> p n t"),
                    op=ALU.mult,
                )

        zq = {}
        tt = {}
        ee = {}

        def zquant(r2):
            zw = work.tile([128, 256], U32, name="zw", align_bytes=64)
            zsc = work.tile([128, 256], U8, name="zsc", align_bytes=64)
            nc.vector.quantize_mx(
                out=zw[:].bitcast(FP8X4), scales=zsc[:], in_=zg[r2][:].rearrange("p j n t -> p (j n t)")
            )
            zq[r2] = (zw, zsc)

        ops = {}

        def omm(n):
            zw, zsc = zq[n // 2]
            j = n % 2
            o = ps_o.tile([128, H], F32, name="o")
            nc.tensor.matmul_mx(
                out=o[:],
                lhsT=zw[:, 128 * j : 128 * j + 128].bitcast(FP8X4),
                lhsT_scale=zsc[:, 128 * j : 128 * j + 128],
                rhs=ww[:].bitcast(FP4X4),
                rhs_scale=ws[:],
                start=True,
                stop=True,
            )
            ops[n] = o

        def bias(n):
            tn = keep.tile([128, H], F32, name="t%d" % n)
            nc.vector.tensor_tensor(out=tn[:], in0=ops[n][:], in1=bb[:], op=ALU.add)
            tcl = work.tile([128, H], F32, name="tcl")
            nc.vector.tensor_scalar_min(out=tcl[:], in0=tn[:], scalar1=T_CLAMP)
            tt[n] = (tn, tcl)

        def eexp(n):
            tn, tcl = tt[n]
            en = keep.tile([128, H], F32, name="en%d" % n)
            nc.scalar.activation(out=en[:], in_=tcl[:], func=ACT.Exp)
            ee[n] = en

        def final(n):
            ln = work.tile([128, H], F32, name="ln", bufs=3)
            nc.scalar.activation(out=ln[:], in_=ee[n][:], func=ACT.Ln, bias=1.0)
            res = work.tile([128, H], F32, name="res", bufs=3)
            nc.vector.tensor_tensor(out=res[:], in0=ln[:], in1=tt[n][0][:], op=ALU.max)
            nc.sync.dma_start(out=out[128 * n : 128 * n + 128, :], in_=res[:])

        vq = []
        for f in feat_parts(0):
            f()
        for hh in range(2):
            for t in range(4):
                for e in range(2):
                    squares(0, 256 * hh, 256 * hh + 256, t, e)
        J = len(jobs)
        pend = []
        late = {}

        def at(it, fn):
            late.setdefault(it, []).append(fn)

        for it in range(J + 12):
            if it < J:
                s = it // CH
                d2_min(it)
                if s + 1 < len(steps):
                    for x in range(2):
                        q = 2 * (it % CH) + x
                        squares(s + 1, 0, CH * 128, q // 2, q % 2)
            if it >= 1 and it - 1 < J:
                expo(it - 1)
            if it >= 3 and it % 2 == 1 and (it - 3) // 2 < J // 2:
                norm((it - 3) // 2)
            for fn in late.pop(it, []):
                fn()
            if it >= 4 and it % 2 == 0 and (it - 4) // 2 < J // 2:
                r = (it - 4) // 2
                xpose(r)
                at(it + 1, lambda r=r: (quant(r), mx(r, 0)))
                at(it + 2, lambda r=r: (mx(r, 1), zmul(2 * r)))
                at(it + 3, lambda r=r: zmul(2 * r + 1))
                c, pl, i = jobs[2 * r]
                if pl == 2:
                    n = c * CH + i
                    at(it + 4, lambda n=n: (zquant(n // 2), omm(n)))
                    at(it + 5, lambda n=n: (bias(n), omm(n + 1)))
                    at(it + 6, lambda n=n: (eexp(n), bias(n + 1)))
                    at(it + 7, lambda n=n: eexp(n + 1))
            if it in (0, 4):
                pend = feat_parts(1 + it // 4)
            for x in range(2):
                if pend:
                    pend.pop(0)()
        for it in sorted(late):
            for fn in late[it]:
                fn()
        for n in range(NT):
            final(n)
